import numpy as np
import ml_dtypes


def mxq(x, axis, fmt="e4m3"):
    dtype, down = {"e4m3": (ml_dtypes.float8_e4m3fn, 7), "e5m2": (ml_dtypes.float8_e5m2, 14)}[fmt]
    v = np.moveaxis(np.asarray(x, np.float32).astype(ml_dtypes.bfloat16).astype(np.float64), axis, -1)
    blocks = v.reshape(v.shape[:-1] + (-1, 32))
    amax = np.abs(blocks).max(-1, keepdims=True)
    byte = np.maximum(np.where(amax > 0, np.frexp(amax)[1] - 1 + 127, 0) - down, 1)
    scale = np.exp2(byte - 127.0)
    codes = (blocks / scale).astype(np.float32).astype(dtype).astype(np.float64)
    return np.moveaxis((codes * scale).reshape(v.shape), -1, axis)


WIDE = False


def mx_kscale(k):
    if not WIDE:
        return np.ones(k)
    levels = np.array([10, -10, 5, -5, 0])
    if k % 512:
        return np.exp2(np.random.permutation(np.resize(levels, k // 32))).repeat(32)
    a = np.empty((k // 512, 16))
    for p in range(k // 512):
        a[p, :8] = np.random.permutation(np.resize(levels, 8))
        for g in range(8):
            far = levels[np.abs(levels - a[p, g]) >= 10]
            a[p, g + 8] = far[np.random.randint(len(far))]
    return np.exp2(a.ravel()).repeat(32)


def f64(x):
    return np.asarray(x).astype(np.float64)


E2M1 = np.array([0.0, 0.5, 1.0, 1.5, 2.0, 3.0, 4.0, 6.0, -0.0, -0.5, -1.0, -1.5, -2.0, -3.0, -4.0, -6.0])


def pack_weight(w, fmt):
    k, n = w.shape
    w = f64(np.asarray(w, np.float32).astype(ml_dtypes.bfloat16)).reshape(k // 32, 32, n)
    amax = np.abs(w).max(1)
    if fmt == "e4m3":
        byte = np.frexp(amax)[1] - 1 + 127 - 7
    else:
        mant, ex = np.frexp(amax / 6.0)
        byte = np.where(mant > 0.5, ex, ex - 1) + 127
    byte = np.clip(np.where(amax > 0, byte, 1), 1, 254)
    scaled = (w * np.exp2(127.0 - byte)[:, None, :]).reshape(k, n).astype(np.float32)
    by_word = np.ascontiguousarray(scaled.reshape(k // 512, 128, 4, n).transpose(0, 1, 3, 2))
    if fmt == "e4m3":
        words = by_word.astype(ml_dtypes.float8_e4m3fn).view(np.uint8)
    else:
        c = by_word.astype(ml_dtypes.float4_e2m1fn).view(np.uint8) & 0xF
        words = (c[..., 0::2] | (c[..., 1::2] << 4)).reshape(k // 512, 128, 2 * n)
    return np.ascontiguousarray(words), np.ascontiguousarray(byte.astype(np.uint8).reshape(k // 512, 16, n))


def unpack_weight(words, scales, fmt):
    g, _, n = scales.shape
    words = np.ascontiguousarray(words).reshape(g, 128, n, -1)
    if fmt == "e4m3":
        vals = words.view(ml_dtypes.float8_e4m3fn).astype(np.float64)
    else:
        nib = np.empty((g, 128, n, 4), np.uint8)
        nib[..., 0::2] = words & 0xF
        nib[..., 1::2] = words >> 4
        vals = E2M1[nib]
    vals = vals * np.repeat(np.exp2(scales.astype(np.float64) - 127.0), 8, axis=1)[..., None]
    return vals.transpose(0, 1, 3, 2).reshape(g * 512, n)


def bf(x):
    return np.asarray(x, np.float32).astype(ml_dtypes.bfloat16)


def planes(Y):
    r, m = Y.shape
    b = f64(bf(Y)).reshape(r // 32, 32, m)
    amax = np.abs(b).max(1)
    byte = np.clip(np.where(amax > 0, np.frexp(amax)[1] - 1 + 127 - 7, 1), 1, 254)
    codes = (b * np.exp2(127.0 - byte)[:, None, :]).reshape(r, m).astype(np.float32).astype(ml_dtypes.float8_e4m3fn).view(np.uint8)
    words = codes.reshape(r // 512, 128, 4, m).transpose(0, 1, 3, 2)
    return np.ascontiguousarray(words), np.ascontiguousarray(byte.astype(np.uint8).reshape(r // 512, 16, m))


K, L, T, R, N = 1024, 512, 512, 512, 512


def setup_inputs():
    n = np.random.standard_normal
    fk = mx_kscale(K)
    fl = mx_kscale(L)
    fr = mx_kscale(R)
    xtp = pack_weight(n((K, T)) / fk[:, None], "e2m1")
    wap = pack_weight(n((K, R)) * 1 / np.sqrt(K) * fk[:, None], "e4m3")
    xqp = pack_weight(n((L, T)) / fl[:, None], "e2m1")
    wcp = pack_weight(n((L, R)) * 1 / np.sqrt(L) * fl[:, None], "e4m3")
    wbp = pack_weight(n((R, N)) * 1 / np.sqrt(R) / fr[:, None], "e2m1")
    wdp = pack_weight(n((R, N)) * 1 / np.sqrt(R) / fr[:, None], "e4m3")
    return {
        "xt_words": xtp[0],
        "xt_scales": xtp[1],
        "wa_words": wap[0],
        "wa_scales": wap[1],
        "xq_words": xqp[0],
        "xq_scales": xqp[1],
        "wc_words": wcp[0],
        "wc_scales": wcp[1],
        "us": (np.random.uniform(0.5, 2.0, (R, 1)) * fr[:, None]).astype(np.float32),
        "ur": (np.random.uniform(0.5, 2.0, (R, 1)) * fr[:, None]).astype(np.float32),
        "wb_words": wbp[0],
        "wb_scales": wbp[1],
        "wd_words": wdp[0],
        "wd_scales": wdp[1],
    }


def reference(xt_words, xt_scales, wa_words, wa_scales, xq_words, xq_scales, wc_words, wc_scales, us, ur, wb_words, wb_scales, wd_words, wd_scales):
    xtu = unpack_weight(xt_words, xt_scales, "e2m1")
    wau = unpack_weight(wa_words, wa_scales, "e4m3")
    xqu = unpack_weight(xq_words, xq_scales, "e2m1")
    wcu = unpack_weight(wc_words, wc_scales, "e4m3")
    wbu = unpack_weight(wb_words, wb_scales, "e2m1")
    wdu = unpack_weight(wd_words, wd_scales, "e4m3")
    z = wau.T @ xtu + wcu.T @ xqu
    ha = 0.5 * np.square(z) * f64(us)
    hb = z * f64(ur)
    haq = mxq(ha, 0, "e4m3")
    hbq = mxq(hb, 0, "e4m3")
    y = wbu.T @ haq + wdu.T @ hbq
    words, scales = planes(y)
    return y, words, scales

@@ -1,0 +1,227 @@
+from contextlib import ExitStack
+
+import concourse.mybir as mybir
+
+K, L, T, R, N = 1024, 512, 512, 512, 512
+FLOPS = 2 * T * R * (K + L) + 2 * 2 * N * T * R
+
+F32 = mybir.dt.float32
+BF16 = mybir.dt.bfloat16
+I32 = mybir.dt.int32
+U32 = mybir.dt.uint32
+U16 = mybir.dt.uint16
+U8 = mybir.dt.uint8
+FP8X4 = mybir.dt.float8_e4m3fn_x4
+FP4X4 = mybir.dt.float4_e2m1fn_x4
+ACT = mybir.ActivationFunctionType
+ALU = mybir.AluOpType
+
+P = 128
+PACK = 4
+W = 512
+TC = 128
+CHUNKS = T // TC
+LINE = 16
+
+
+def tile_mix_hidden_squares_and_values_pl_kernel(
+    tc, xt_words, xt_scales, wa_words, wa_scales, xq_words, xq_scales, wc_words, wc_scales,
+    us, ur, wb_words, wb_scales, wd_words, wd_scales, out_0, out_1, out_2,
+):
+    nc = tc.nc
+    with ExitStack() as ctx:
+        sb = ctx.enter_context(tc.tile_pool(name="sb", bufs=1))
+        ps = ctx.enter_context(tc.psum_pool(name="ps", bufs=1))
+        ctx.enter_context(tc.manual_schedule())
+
+        def new(name, shape, dtype):
+            return sb.tile(shape, dtype, name=name, align_bytes=64)
+
+        def load_fp8(queue, name, words):
+            raw = new(name, [P, W], U32)
+            queue.dma_start(out=raw[:].bitcast(I32), in_=words.rearrange("p n t -> p (n t)").bitcast(I32))
+            return raw
+
+        def load_fp4(queue, name, words):
+            raw = new(name, [P, W], U16)
+            queue.dma_start(out=raw[:].bitcast(I32), in_=words.bitcast(I32))
+            return raw
+
+        def deal(copy, name, raw, dtype, run):
+            dealt = new(name, [P, PACK, P], dtype)
+            copy(out=dealt[:].rearrange("p j (c i) -> p c j i", i=run), in_=raw.rearrange("p (c i j) -> p c j i", i=run, j=PACK))
+            return dealt
+
+        planes = new("planes", [P, 6, W], U8)
+        planes2 = new("planes2", [P, 2, W], U8)
+        nc.vector.memset(planes[:].rearrange("p s c -> p (s c)").bitcast(U32), 0)
+        nc.vector.memset(planes2[:].rearrange("p s c -> p (s c)").bitcast(U32), 0)
+        staged = new("staged", [32, 6, W], U8)
+        slot = 0
+        for scales in (wa_scales, wc_scales, xt_scales, xq_scales):
+            passes = scales.shape[0]
+            nc.scalar.dma_start(
+                out=staged[16:32, slot:slot + passes, :].bitcast(I32),
+                in_=scales.rearrange("z q c -> q z c").bitcast(I32),
+            )
+            slot += passes
+        wa_raw = new("wa_raw", [P, 2, W], U32)
+        nc.sync.dma_start(out=wa_raw[:].bitcast(I32), in_=wa_words.rearrange("z p n t -> p z (n t)").bitcast(I32))
+        wc_raw = load_fp8(nc.sync, "wc_raw", wc_words[0])
+        xt_half, xq_half = [], []
+
+        def load_x(h):
+            cols = slice(h * W, (h + 1) * W)
+            xt_h = new("xt_half%d" % h, [P, 2, W // 2], U16)
+            xq_h = new("xq_half%d" % h, [P, W // 2], U16)
+            nc.sync.dma_start(out=xt_h[:].bitcast(I32), in_=xt_words[:, :, cols].rearrange("z p b -> p z b").bitcast(I32))
+            nc.sync.dma_start(out=xq_h[:].bitcast(I32), in_=xq_words[0, :, cols].bitcast(I32))
+            xt_half.append(xt_h)
+            xq_half.append(xq_h)
+
+        load_x(0)
+        us_sb = new("us_sb", [P, PACK], F32)
+        ur_sb = new("ur_sb", [P, PACK], F32)
+        nc.gpsimd.dma_start(out=us_sb[:], in_=us.rearrange("(p j) o -> p (j o)", j=PACK))
+        nc.gpsimd.dma_start(out=ur_sb[:], in_=ur.rearrange("(p j) o -> p (j o)", j=PACK))
+        for q in range(4):
+            nc.scalar.dma_start(
+                out=planes[32 * q:32 * q + 4].rearrange("p s c -> p (s c)").bitcast(I32),
+                in_=staged[16 + 4 * q:20 + 4 * q].rearrange("p s c -> p (s c)").bitcast(I32),
+            )
+        load_x(1)
+        wd_raw = load_fp8(nc.sync, "wd_raw", wd_words[0])
+        wb_raw = load_fp4(nc.sync, "wb_raw", wb_words[0])
+        for slot, scales in enumerate((wd_scales, wb_scales)):
+            for q in range(4):
+                nc.sync.dma_start(out=planes2[32 * q:32 * q + 4, slot, :].bitcast(I32), in_=scales[0, 4 * q:4 * q + 4, :].bitcast(I32))
+
+        w_codes = [
+            deal(nc.vector.tensor_copy, "w_codes0", wa_raw[:, 0, :], U32, LINE // 4),
+            deal(nc.scalar.copy, "w_codes1", wa_raw[:, 1, :], U32, LINE // 4),
+            deal(nc.vector.tensor_copy, "w_codes2", wc_raw[:], U32, LINE // 4),
+        ]
+        half_us = new("half_us", [P, PACK], F32)
+        nc.scalar.activation(out=half_us[:], in_=us_sb[:], func=ACT.Copy, scale=0.5)
+        w_scales = [deal(nc.vector.tensor_copy, "w_scales%d" % g, planes[:, g, :], U8, LINE) for g in range(3)]
+        z = [ps.tile([P, PACK, TC], F32, name="z%d" % c) for c in range(CHUNKS)]
+        y = [ps.tile([P, PACK, TC], F32, name="y%d" % c) for c in range(CHUNKS)]
+
+        def first_layer(c):
+            half, lo = divmod(c * TC, W // 2)
+            x_codes = [xt_half[half][:, 0, lo:lo + TC], xt_half[half][:, 1, lo:lo + TC], xq_half[half][:, lo:lo + TC]]
+            for g in range(3):
+                for j in range(PACK):
+                    nc.tensor.matmul_mx(
+                        out=z[c][:, j, :],
+                        lhsT=w_codes[g][:, j, :].bitcast(FP8X4), lhsT_scale=w_scales[g][:, j, :],
+                        rhs=x_codes[g].bitcast(FP4X4), rhs_scale=planes[:, 3 + g, c * TC:(c + 1) * TC],
+                        start=(g == 0 and j == 0), stop=(g == 2 and j == PACK - 1),
+                    )
+
+
+        sq = [new("sq%d" % c, [P, TC, PACK], F32) for c in range(CHUNKS)]
+        ha = [new("ha%d" % c, [P, TC, PACK], BF16) for c in range(CHUNKS)]
+        hb = [new("hb%d" % c, [P, TC, PACK], BF16) for c in range(CHUNKS)]
+        ha_codes = [new("ha_codes%d" % c, [P, TC], U32) for c in range(CHUNKS)]
+        hb_codes = [new("hb_codes%d" % c, [P, TC], U32) for c in range(CHUNKS)]
+        ha_scales = [new("ha_scales%d" % c, [P, TC], U8) for c in range(CHUNKS)]
+        hb_scales = [new("hb_scales%d" % c, [P, TC], U8) for c in range(CHUNKS)]
+        y_f32 = [new("y_f32_%d" % c, [P, PACK, TC], F32) for c in range(CHUNKS)]
+        y_bf = [new("y_bf%d" % c, [P, TC, PACK], BF16) for c in range(CHUNKS)]
+        y_codes = [new("y_codes%d" % c, [P, TC], U32) for c in range(CHUNKS)]
+        y_scales = new("y_scales", [P, T], U8)
+        out_rows = out_0.rearrange("(p i) t -> p i t", i=PACK)
+        out_words = out_1[0].rearrange("p t r -> p (t r)").bitcast(I32)
+
+        def over_t(factors):
+            return factors[:].unsqueeze(1).broadcast_to([P, TC, PACK])
+
+        def make_hb(c):
+            nc.vector.tensor_tensor(out=hb[c][:], in0=z[c][:].rearrange("p j t -> p t j"), in1=over_t(ur_sb), op=ALU.mult)
+
+        def make_sq(c):
+            nc.scalar.activation(out=sq[c][:], in_=z[c][:].rearrange("p j t -> p t j"), func=ACT.Square)
+
+        def make_ha(c):
+            nc.vector.tensor_tensor(out=ha[c][:], in0=sq[c][:], in1=over_t(half_us), op=ALU.mult)
+
+        def quantize(codes, scales, values):
+            nc.vector.quantize_mx(out=codes.bitcast(FP8X4), scales=scales, in_=values[:].rearrange("p t j -> p (t j)"))
+
+        def second_layer(c):
+            for i in range(PACK):
+                nc.tensor.matmul_mx(
+                    out=y[c][:, i, :],
+                    lhsT=wd_codes[:, i, :].bitcast(FP8X4), lhsT_scale=wd_sc[:, i, :],
+                    rhs=hb_codes[c][:].bitcast(FP8X4), rhs_scale=hb_scales[c][:],
+                    start=(i == 0), stop=False,
+                )
+            for i in range(PACK):
+                nc.tensor.matmul_mx(
+                    out=y[c][:, i, :],
+                    lhsT=wb_codes[:, i, :].bitcast(FP4X4), lhsT_scale=wb_sc[:, i, :],
+                    rhs=ha_codes[c][:].bitcast(FP8X4), rhs_scale=ha_scales[c][:],
+                    start=False, stop=(i == PACK - 1),
+                )
+
+        def store_y(c):
+            nc.scalar.copy(out=y_f32[c][:], in_=y[c][:])
+            nc.sync.dma_start(out=out_rows[:, :, c * TC:(c + 1) * TC], in_=y_f32[c][:])
+
+        def round_y_scalar(c):
+            nc.scalar.copy(out=y_bf[c][:], in_=y[c][:].rearrange("p i t -> p t i"))
+
+        def round_y_vector(c):
+            nc.vector.tensor_copy(
+                out=y_bf[c][:].rearrange("p (a b) i -> p a i b", b=4),
+                in_=y_f32[c][:].rearrange("p i (a b) -> p a i b", b=4),
+            )
+
+        def quantize_y(c):
+            cols = slice(c * TC, (c + 1) * TC)
+            quantize(y_codes[c][:], y_scales[:, cols], y_bf[c])
+            nc.sync.dma_start(out=out_words[:, cols], in_=y_codes[c][:].bitcast(I32))
+
+        def hidden(c):
+            make_ha(c)
+            quantize(hb_codes[c][:], hb_scales[c][:], hb[c])
+            quantize(ha_codes[c][:], ha_scales[c][:], ha[c])
+
+        for c in range(CHUNKS):
+            first_layer(c)
+        make_hb(0)
+        make_sq(0)
+        wd_sc = deal(nc.vector.tensor_copy, "wd_sc", planes2[:, 0, :], U8, LINE)
+        wb_sc = deal(nc.vector.tensor_copy, "wb_sc", planes2[:, 1, :], U8, LINE)
+        wd_codes = deal(nc.scalar.copy, "wd_codes", wd_raw[:], U32, LINE // 4)
+        make_hb(1)
+        make_sq(1)
+        wb_codes = deal(nc.scalar.copy, "wb_codes", wb_raw[:], U16, LINE // 2)
+        hidden(0)
+        second_layer(0)
+        make_hb(2)
+        make_sq(2)
+        hidden(1)
+        second_layer(1)
+        store_y(0)
+        round_y_scalar(0)
+        make_hb(3)
+        make_sq(3)
+        hidden(2)
+        second_layer(2)
+        store_y(1)
+        round_y_scalar(1)
+        hidden(3)
+        second_layer(3)
+        store_y(2)
+        quantize_y(0)
+        quantize_y(1)
+        round_y_vector(2)
+        store_y(3)
+        quantize_y(2)
+        round_y_vector(3)
+        quantize_y(3)
+        for q in range(4):
+            queue = nc.sync if q % 2 == 0 else nc.scalar
+            queue.dma_start(out=out_2[0, 4 * q:4 * q + 4, :].bitcast(I32), in_=y_scales[32 * q:32 * q + 4, :].bitcast(I32))

@@ -52,15 +52,14 @@ def tile_mix_hidden_squares_and_values_pl_kernel(
             copy(out=dealt[:].rearrange("p j (c i) -> p c j i", i=run), in_=raw.rearrange("p (c i j) -> p c j i", i=run, j=PACK))
             return dealt
 
-        planes = new("planes", [P, 6, W], U8)
-        planes2 = new("planes2", [P, 2, W], U8)
+        planes = new("planes", [P, 8, W], U8)
         nc.vector.memset(planes[:].rearrange("p s c -> p (s c)").bitcast(U32), 0)
-        nc.vector.memset(planes2[:].rearrange("p s c -> p (s c)").bitcast(U32), 0)
-        staged = new("staged", [32, 6, W], U8)
+        staged = new("staged", [32, 8, W], U8)
         slot = 0
-        for scales in (wa_scales, wc_scales, xt_scales, xq_scales):
+        for n, scales in enumerate((wa_scales, xt_scales, wc_scales, xq_scales, wd_scales, wb_scales)):
             passes = scales.shape[0]
-            nc.scalar.dma_start(
+            queue = nc.sync if n % 2 == 0 else nc.scalar
+            queue.dma_start(
                 out=staged[16:32, slot:slot + passes, :].bitcast(I32),
                 in_=scales.rearrange("z q c -> q z c").bitcast(I32),
             )
@@ -68,9 +67,17 @@ def tile_mix_hidden_squares_and_values_pl_kernel(
         wa_raw = new("wa_raw", [P, 2, W], U32)
         nc.sync.dma_start(out=wa_raw[:].bitcast(I32), in_=wa_words.rearrange("z p n t -> p z (n t)").bitcast(I32))
         wc_raw = load_fp8(nc.sync, "wc_raw", wc_words[0])
-        xt_half, xq_half = [], []
+        us_sb = new("us_sb", [P, PACK], F32)
+        ur_sb = new("ur_sb", [P, PACK], F32)
 
-        def load_x(h):
+        for q in range(4):
+            queue = nc.sync if q % 2 == 0 else nc.scalar
+            queue.dma_start(
+                out=planes[32 * q:32 * q + 4].rearrange("p s c -> p (s c)").bitcast(I32),
+                in_=staged[16 + 4 * q:20 + 4 * q].rearrange("p s c -> p (s c)").bitcast(I32),
+            )
+        xt_half, xq_half = [], []
+        for h in range(2):
             cols = slice(h * W, (h + 1) * W)
             xt_h = new("xt_half%d" % h, [P, 2, W // 2], U16)
             xq_h = new("xq_half%d" % h, [P, W // 2], U16)
@@ -78,32 +85,17 @@ def tile_mix_hidden_squares_and_values_pl_kernel(
             nc.sync.dma_start(out=xq_h[:].bitcast(I32), in_=xq_words[0, :, cols].bitcast(I32))
             xt_half.append(xt_h)
             xq_half.append(xq_h)
-
-        load_x(0)
-        us_sb = new("us_sb", [P, PACK], F32)
-        ur_sb = new("ur_sb", [P, PACK], F32)
-        nc.gpsimd.dma_start(out=us_sb[:], in_=us.rearrange("(p j) o -> p (j o)", j=PACK))
-        nc.gpsimd.dma_start(out=ur_sb[:], in_=ur.rearrange("(p j) o -> p (j o)", j=PACK))
-        for q in range(4):
-            nc.scalar.dma_start(
-                out=planes[32 * q:32 * q + 4].rearrange("p s c -> p (s c)").bitcast(I32),
-                in_=staged[16 + 4 * q:20 + 4 * q].rearrange("p s c -> p (s c)").bitcast(I32),
-            )
-        load_x(1)
         wd_raw = load_fp8(nc.sync, "wd_raw", wd_words[0])
         wb_raw = load_fp4(nc.sync, "wb_raw", wb_words[0])
-        for slot, scales in enumerate((wd_scales, wb_scales)):
-            for q in range(4):
-                nc.sync.dma_start(out=planes2[32 * q:32 * q + 4, slot, :].bitcast(I32), in_=scales[0, 4 * q:4 * q + 4, :].bitcast(I32))
+        nc.sync.dma_start(out=ur_sb[:], in_=ur.rearrange("(p j) o -> p (j o)", j=PACK))
+        nc.sync.dma_start(out=us_sb[:], in_=us.rearrange("(p j) o -> p (j o)", j=PACK))
 
         w_codes = [
             deal(nc.vector.tensor_copy, "w_codes0", wa_raw[:, 0, :], U32, LINE // 4),
-            deal(nc.scalar.copy, "w_codes1", wa_raw[:, 1, :], U32, LINE // 4),
+            deal(nc.vector.tensor_copy, "w_codes1", wa_raw[:, 1, :], U32, LINE // 4),
             deal(nc.vector.tensor_copy, "w_codes2", wc_raw[:], U32, LINE // 4),
         ]
-        half_us = new("half_us", [P, PACK], F32)
-        nc.scalar.activation(out=half_us[:], in_=us_sb[:], func=ACT.Copy, scale=0.5)
-        w_scales = [deal(nc.vector.tensor_copy, "w_scales%d" % g, planes[:, g, :], U8, LINE) for g in range(3)]
+        w_scales = [deal(nc.vector.tensor_copy, "w_scales%d" % g, planes[:, (0, 1, 4)[g], :], U8, LINE) for g in range(3)]
         z = [ps.tile([P, PACK, TC], F32, name="z%d" % c) for c in range(CHUNKS)]
         y = [ps.tile([P, PACK, TC], F32, name="y%d" % c) for c in range(CHUNKS)]
 
@@ -115,7 +107,7 @@ def tile_mix_hidden_squares_and_values_pl_kernel(
                     nc.tensor.matmul_mx(
                         out=z[c][:, j, :],
                         lhsT=w_codes[g][:, j, :].bitcast(FP8X4), lhsT_scale=w_scales[g][:, j, :],
-                        rhs=x_codes[g].bitcast(FP4X4), rhs_scale=planes[:, 3 + g, c * TC:(c + 1) * TC],
+                        rhs=x_codes[g].bitcast(FP4X4), rhs_scale=planes[:, (2, 3, 5)[g], c * TC:(c + 1) * TC],
                         start=(g == 0 and j == 0), stop=(g == 2 and j == PACK - 1),
                     )
 
@@ -129,7 +121,8 @@ def tile_mix_hidden_squares_and_values_pl_kernel(
         hb_scales = [new("hb_scales%d" % c, [P, TC], U8) for c in range(CHUNKS)]
         y_f32 = [new("y_f32_%d" % c, [P, PACK, TC], F32) for c in range(CHUNKS)]
         y_bf = [new("y_bf%d" % c, [P, TC, PACK], BF16) for c in range(CHUNKS)]
-        y_codes = [new("y_codes%d" % c, [P, TC], U32) for c in range(CHUNKS)]
+        y_codes = new("y_codes", [P, T], U32)
+        hb_rows = [new("hb_rows%d" % c, [P, PACK, TC], BF16) for c in range(CHUNKS)]
         y_scales = new("y_scales", [P, T], U8)
         out_rows = out_0.rearrange("(p i) t -> p i t", i=PACK)
         out_words = out_1[0].rearrange("p t r -> p (t r)").bitcast(I32)
@@ -144,25 +137,27 @@ def tile_mix_hidden_squares_and_values_pl_kernel(
             nc.scalar.activation(out=sq[c][:], in_=z[c][:].rearrange("p j t -> p t j"), func=ACT.Square)
 
         def make_ha(c):
-            nc.vector.tensor_tensor(out=ha[c][:], in0=sq[c][:], in1=over_t(half_us), op=ALU.mult)
+            nc.vector.scalar_tensor_tensor(out=ha[c][:], in0=sq[c][:], scalar=0.5, in1=over_t(us_sb), op0=ALU.mult, op1=ALU.mult)
 
         def quantize(codes, scales, values):
             nc.vector.quantize_mx(out=codes.bitcast(FP8X4), scales=scales, in_=values[:].rearrange("p t j -> p (t j)"))
 
-        def second_layer(c):
+        def second_values(c, first):
             for i in range(PACK):
                 nc.tensor.matmul_mx(
                     out=y[c][:, i, :],
                     lhsT=wd_codes[:, i, :].bitcast(FP8X4), lhsT_scale=wd_sc[:, i, :],
                     rhs=hb_codes[c][:].bitcast(FP8X4), rhs_scale=hb_scales[c][:],
-                    start=(i == 0), stop=False,
+                    start=(first and i == 0), stop=(not first and i == PACK - 1),
                 )
+
+        def second_squares(c, first):
             for i in range(PACK):
                 nc.tensor.matmul_mx(
                     out=y[c][:, i, :],
                     lhsT=wb_codes[:, i, :].bitcast(FP4X4), lhsT_scale=wb_sc[:, i, :],
                     rhs=ha_codes[c][:].bitcast(FP8X4), rhs_scale=ha_scales[c][:],
-                    start=False, stop=(i == PACK - 1),
+                    start=(first and i == 0), stop=(not first and i == PACK - 1),
                 )
 
         def store_y(c):
@@ -180,48 +175,59 @@ def tile_mix_hidden_squares_and_values_pl_kernel(
 
         def quantize_y(c):
             cols = slice(c * TC, (c + 1) * TC)
-            quantize(y_codes[c][:], y_scales[:, cols], y_bf[c])
-            nc.sync.dma_start(out=out_words[:, cols], in_=y_codes[c][:].bitcast(I32))
+            quantize(y_codes[:, cols], y_scales[:, cols], y_bf[c])
 
-        def hidden(c):
-            make_ha(c)
-            quantize(hb_codes[c][:], hb_scales[c][:], hb[c])
+        def store_codes(cols):
+            nc.sync.dma_start(out=out_words[:, cols], in_=y_codes[:, cols].bitcast(I32))
+
+        def make_hb_rows(c):
+            for j in range(PACK):
+                nc.scalar.activation(out=hb_rows[c][:, j, :], in_=z[c][:, j, :], func=ACT.Copy, scale=ur_sb[:, j:j + 1])
+
+        def interleave_hb(c):
+            nc.vector.tensor_copy(
+                out=hb[c][:].rearrange("p (a b) j -> p a j b", b=4),
+                in_=hb_rows[c][:].rearrange("p j (a b) -> p a j b", b=4),
+            )
+
+        def qa(c):
             quantize(ha_codes[c][:], ha_scales[c][:], ha[c])
 
+        def qb(c):
+            quantize(hb_codes[c][:], hb_scales[c][:], hb[c])
+
+        wd_sc = deal(nc.vector.tensor_copy, "wd_sc", planes[:, 6, :], U8, LINE)
+        wb_sc = deal(nc.vector.tensor_copy, "wb_sc", planes[:, 7, :], U8, LINE)
+        wd_codes = deal(nc.vector.tensor_copy, "wd_codes", wd_raw[:], U32, LINE // 4)
+        wb_codes = deal(nc.vector.tensor_copy, "wb_codes", wb_raw[:], U16, LINE // 2)
         for c in range(CHUNKS):
             first_layer(c)
-        make_hb(0)
-        make_sq(0)
-        wd_sc = deal(nc.vector.tensor_copy, "wd_sc", planes2[:, 0, :], U8, LINE)
-        wb_sc = deal(nc.vector.tensor_copy, "wb_sc", planes2[:, 1, :], U8, LINE)
-        wd_codes = deal(nc.scalar.copy, "wd_codes", wd_raw[:], U32, LINE // 4)
-        make_hb(1)
-        make_sq(1)
-        wb_codes = deal(nc.scalar.copy, "wb_codes", wb_raw[:], U16, LINE // 2)
-        hidden(0)
-        second_layer(0)
-        make_hb(2)
-        make_sq(2)
-        hidden(1)
-        second_layer(1)
+        for c in range(CHUNKS):
+            make_sq(c)
+            make_hb_rows(c)
+            make_ha(c)
+            if c > 0:
+                qb(c - 1)
+                second_values(c - 1, False)
+            interleave_hb(c)
+            qa(c)
+            second_squares(c, True)
+        qb(3)
+        second_values(3, False)
         store_y(0)
-        round_y_scalar(0)
-        make_hb(3)
-        make_sq(3)
-        hidden(2)
-        second_layer(2)
         store_y(1)
-        round_y_scalar(1)
-        hidden(3)
-        second_layer(3)
         store_y(2)
+        round_y_vector(0)
+        round_y_vector(1)
         quantize_y(0)
         quantize_y(1)
         round_y_vector(2)
         store_y(3)
         quantize_y(2)
+        store_codes(slice(0, 3 * TC))
         round_y_vector(3)
         quantize_y(3)
+        store_codes(slice(3 * TC, T))
         for q in range(4):
             queue = nc.sync if q % 2 == 0 else nc.scalar
             queue.dma_start(out=out_2[0, 4 * q:4 * q + 4, :].bitcast(I32), in_=y_scales[32 * q:32 * q + 4, :].bitcast(I32))

@@ -18,10 +18,16 @@ ALU = mybir.AluOpType
 
 P = 128
 PACK = 4
-W = 512
-TC = 128
-CHUNKS = T // TC
+WIDTH = 512
+CHUNK = 128
+CHUNKS = T // CHUNK
+LAST = CHUNKS - 1
+HALF = T // 2
 LINE = 16
+RUN = 4
+QUADRANT = 32
+SCALE_ROWS = 16
+WA, XT, WC, XQ, WD, WB, SCALE_PASSES = 0, 2, 4, 5, 6, 7, 8
 
 
 def tile_mix_hidden_squares_and_values_pl_kernel(
@@ -37,197 +43,215 @@ def tile_mix_hidden_squares_and_values_pl_kernel(
         def new(name, shape, dtype):
             return sb.tile(shape, dtype, name=name, align_bytes=64)
 
-        def load_fp8(queue, name, words):
-            raw = new(name, [P, W], U32)
-            queue.dma_start(out=raw[:].bitcast(I32), in_=words.rearrange("p n t -> p (n t)").bitcast(I32))
-            return raw
+        def per_chunk(name, shape, dtype, count=CHUNKS):
+            return [new("%s%d" % (name, c), shape, dtype) for c in range(count)]
 
-        def load_fp4(queue, name, words):
-            raw = new(name, [P, W], U16)
-            queue.dma_start(out=raw[:].bitcast(I32), in_=words.bitcast(I32))
-            return raw
+        def load_words(name, shape, dtype, source):
+            tile = new(name, shape, dtype)
+            nc.sync.dma_start(out=tile[:].bitcast(I32), in_=source.bitcast(I32))
+            return tile
 
-        def deal(copy, name, raw, dtype, run):
-            dealt = new(name, [P, PACK, P], dtype)
-            copy(out=dealt[:].rearrange("p j (c i) -> p c j i", i=run), in_=raw.rearrange("p (c i j) -> p c j i", i=run, j=PACK))
+        def load_factors(name, source):
+            tile = new(name, [P, PACK], F32)
+            nc.sync.dma_start(out=tile[:], in_=source.rearrange("(p j) o -> p (j o)", j=PACK))
+            return tile
+
+        def load_xt(half):
+            source = xt_words[:, :, 2 * HALF * half:2 * HALF * (half + 1)].rearrange("z p b -> p z b")
+            return load_words("xt%d" % half, [P, 2, HALF], U16, source)
+
+        def load_xq(half):
+            return load_words("xq%d" % half, [P, HALF], U16, xq_words[0, :, 2 * HALF * half:2 * HALF * (half + 1)])
+
+        def deal(copy, name, raw, item_bytes):
+            dealt = new(name, [P, PACK, P], raw.dtype)
+            run = LINE // item_bytes
+            copy(
+                out=dealt[:].rearrange("p j (c i) -> p c j i", i=run),
+                in_=raw.rearrange("p (c i j) -> p c j i", i=run, j=PACK),
+            )
             return dealt
 
-        planes = new("planes", [P, 8, W], U8)
-        nc.vector.memset(planes[:].rearrange("p s c -> p (s c)").bitcast(U32), 0)
-        staged = new("staged", [32, 8, W], U8)
-        slot = 0
-        for n, scales in enumerate((wa_scales, xt_scales, wc_scales, xq_scales, wd_scales, wb_scales)):
-            passes = scales.shape[0]
-            queue = nc.sync if n % 2 == 0 else nc.scalar
-            queue.dma_start(
-                out=staged[16:32, slot:slot + passes, :].bitcast(I32),
-                in_=scales.rearrange("z q c -> q z c").bitcast(I32),
+        scales = new("scales", [P, SCALE_PASSES, WIDTH], U8)
+        nc.vector.memset(scales[:].rearrange("p s c -> p (s c)").bitcast(U32), 0)
+        staged = new("staged", [2 * SCALE_ROWS, SCALE_PASSES, WIDTH], U8)
+        queues = (nc.sync, nc.scalar)
+        sources = ((WA, wa_scales), (XT, xt_scales), (WC, wc_scales), (XQ, xq_scales), (WD, wd_scales), (WB, wb_scales))
+        for number, (place, source) in enumerate(sources):
+            queues[number % 2].dma_start(
+                out=staged[SCALE_ROWS:, place:place + source.shape[0], :].bitcast(I32),
+                in_=source.rearrange("z q c -> q z c").bitcast(I32),
             )
-            slot += passes
-        wa_raw = new("wa_raw", [P, 2, W], U32)
-        nc.sync.dma_start(out=wa_raw[:].bitcast(I32), in_=wa_words.rearrange("z p n t -> p z (n t)").bitcast(I32))
-        wc_raw = load_fp8(nc.sync, "wc_raw", wc_words[0])
-        us_sb = new("us_sb", [P, PACK], F32)
-        ur_sb = new("ur_sb", [P, PACK], F32)
-
-        for q in range(4):
-            queue = nc.sync if q % 2 == 0 else nc.scalar
-            queue.dma_start(
-                out=planes[32 * q:32 * q + 4].rearrange("p s c -> p (s c)").bitcast(I32),
-                in_=staged[16 + 4 * q:20 + 4 * q].rearrange("p s c -> p (s c)").bitcast(I32),
+        wa_raw = load_words("wa_raw", [P, 2, WIDTH], U32, wa_words.rearrange("z p n t -> p z (n t)"))
+        xt = [load_xt(0)]
+        for row in range(4):
+            queues[row % 2].dma_start(
+                out=scales[row:P:QUADRANT].rearrange("p s c -> p (s c)").bitcast(I32),
+                in_=staged[SCALE_ROWS + row::4].rearrange("p s c -> p (s c)").bitcast(I32),
             )
-        xt_half, xq_half = [], []
-        for h in range(2):
-            cols = slice(h * W, (h + 1) * W)
-            xt_h = new("xt_half%d" % h, [P, 2, W // 2], U16)
-            xq_h = new("xq_half%d" % h, [P, W // 2], U16)
-            nc.sync.dma_start(out=xt_h[:].bitcast(I32), in_=xt_words[:, :, cols].rearrange("z p b -> p z b").bitcast(I32))
-            nc.sync.dma_start(out=xq_h[:].bitcast(I32), in_=xq_words[0, :, cols].bitcast(I32))
-            xt_half.append(xt_h)
-            xq_half.append(xq_h)
-        wd_raw = load_fp8(nc.sync, "wd_raw", wd_words[0])
-        wb_raw = load_fp4(nc.sync, "wb_raw", wb_words[0])
-        nc.sync.dma_start(out=ur_sb[:], in_=ur.rearrange("(p j) o -> p (j o)", j=PACK))
-        nc.sync.dma_start(out=us_sb[:], in_=us.rearrange("(p j) o -> p (j o)", j=PACK))
+        ur_sb = load_factors("ur_sb", ur)
+        us_sb = load_factors("us_sb", us)
+        wc_raw = load_words("wc_raw", [P, WIDTH], U32, wc_words[0].rearrange("p n t -> p (n t)"))
+        xq = [load_xq(0)]
+        wb_raw = load_words("wb_raw", [P, WIDTH], U16, wb_words[0])
+        wd_raw = load_words("wd_raw", [P, WIDTH], U32, wd_words[0].rearrange("p n t -> p (n t)"))
+        xt.append(load_xt(1))
+        xq.append(load_xq(1))
 
-        w_codes = [
-            deal(nc.vector.tensor_copy, "w_codes0", wa_raw[:, 0, :], U32, LINE // 4),
-            deal(nc.vector.tensor_copy, "w_codes1", wa_raw[:, 1, :], U32, LINE // 4),
-            deal(nc.vector.tensor_copy, "w_codes2", wc_raw[:], U32, LINE // 4),
+        w_codes = [deal(nc.vector.tensor_copy, "wa_codes%d" % g, wa_raw[:, g, :], 4) for g in range(2)]
+        first_scales = new("wa_scales0", [P, PACK, P], U8)
+        for j in range(PACK):
+            nc.vector.tensor_copy(out=first_scales[:, j, :], in_=scales[:, WA, j::PACK])
+        w_scales = [
+            first_scales,
+            deal(nc.vector.tensor_copy, "wa_scales1", scales[:, WA + 1, :], 1),
+            deal(nc.vector.tensor_copy, "wc_scales", scales[:, WC, :], 1),
         ]
-        w_scales = [deal(nc.vector.tensor_copy, "w_scales%d" % g, planes[:, (0, 1, 4)[g], :], U8, LINE) for g in range(3)]
-        z = [ps.tile([P, PACK, TC], F32, name="z%d" % c) for c in range(CHUNKS)]
-        y = [ps.tile([P, PACK, TC], F32, name="y%d" % c) for c in range(CHUNKS)]
+        w_codes.append(deal(nc.vector.tensor_copy, "wc_codes", wc_raw[:], 4))
+        wb_dealt_scales = deal(nc.vector.tensor_copy, "wb_scales", scales[:, WB, :], 1)
+        wd_dealt_scales = deal(nc.vector.tensor_copy, "wd_scales", scales[:, WD, :], 1)
+        wb_codes = deal(nc.vector.tensor_copy, "wb_codes", wb_raw[:], 2)
+        wd_codes = deal(nc.vector.tensor_copy, "wd_codes", wd_raw[:], 4)
 
-        def first_layer(c):
-            half, lo = divmod(c * TC, W // 2)
-            x_codes = [xt_half[half][:, 0, lo:lo + TC], xt_half[half][:, 1, lo:lo + TC], xq_half[half][:, lo:lo + TC]]
-            for g in range(3):
+        z = [ps.tile([P, PACK, CHUNK], F32, name="z%d" % c, tag="z%d" % c) for c in range(CHUNKS)]
+        for c in range(CHUNKS):
+            half, start = divmod(c * CHUNK, HALF)
+            in_half = slice(start, start + CHUNK)
+            x_codes = (xt[half][:, 0, in_half], xt[half][:, 1, in_half], xq[half][:, in_half])
+            for g, x_place in enumerate((XT, XT + 1, XQ)):
                 for j in range(PACK):
                     nc.tensor.matmul_mx(
                         out=z[c][:, j, :],
-                        lhsT=w_codes[g][:, j, :].bitcast(FP8X4), lhsT_scale=w_scales[g][:, j, :],
-                        rhs=x_codes[g].bitcast(FP4X4), rhs_scale=planes[:, (2, 3, 5)[g], c * TC:(c + 1) * TC],
-                        start=(g == 0 and j == 0), stop=(g == 2 and j == PACK - 1),
+                        lhsT=w_codes[g][:, j, :].bitcast(FP8X4),
+                        lhsT_scale=w_scales[g][:, j, :],
+                        rhs=x_codes[g].bitcast(FP4X4),
+                        rhs_scale=scales[:, x_place, c * CHUNK:(c + 1) * CHUNK],
+                        start=(g == 0 and j == 0),
+                        stop=(g == 2 and j == PACK - 1),
                     )
 
-
-        sq = [new("sq%d" % c, [P, TC, PACK], F32) for c in range(CHUNKS)]
-        ha = [new("ha%d" % c, [P, TC, PACK], BF16) for c in range(CHUNKS)]
-        hb = [new("hb%d" % c, [P, TC, PACK], BF16) for c in range(CHUNKS)]
-        ha_codes = [new("ha_codes%d" % c, [P, TC], U32) for c in range(CHUNKS)]
-        hb_codes = [new("hb_codes%d" % c, [P, TC], U32) for c in range(CHUNKS)]
-        ha_scales = [new("ha_scales%d" % c, [P, TC], U8) for c in range(CHUNKS)]
-        hb_scales = [new("hb_scales%d" % c, [P, TC], U8) for c in range(CHUNKS)]
-        y_f32 = [new("y_f32_%d" % c, [P, PACK, TC], F32) for c in range(CHUNKS)]
-        y_bf = [new("y_bf%d" % c, [P, TC, PACK], BF16) for c in range(CHUNKS)]
+        squares = per_chunk("squares", [P, CHUNK, PACK], F32)
+        ha = per_chunk("ha", [P, CHUNK, PACK], BF16)
+        hb = per_chunk("hb", [P, CHUNK, PACK], BF16)
+        hb_rows = per_chunk("hb_rows", [P, PACK, CHUNK], BF16, LAST)
+        ha_codes = per_chunk("ha_codes", [P, CHUNK], U32)
+        hb_codes = per_chunk("hb_codes", [P, CHUNK], U32)
+        ha_scales = per_chunk("ha_scales", [P, CHUNK], U8)
+        hb_scales = per_chunk("hb_scales", [P, CHUNK], U8)
+        y_f32 = per_chunk("y_f32_", [P, PACK, CHUNK], F32)
+        y_bf16 = per_chunk("y_bf16_", [P, CHUNK, PACK], BF16)
         y_codes = new("y_codes", [P, T], U32)
-        hb_rows = [new("hb_rows%d" % c, [P, PACK, TC], BF16) for c in range(CHUNKS)]
         y_scales = new("y_scales", [P, T], U8)
+        y_banks = []
         out_rows = out_0.rearrange("(p i) t -> p i t", i=PACK)
         out_words = out_1[0].rearrange("p t r -> p (t r)").bitcast(I32)
 
-        def over_t(factors):
-            return factors[:].unsqueeze(1).broadcast_to([P, TC, PACK])
+        def tokens(c):
+            return slice(c * CHUNK, (c + 1) * CHUNK)
 
-        def make_hb(c):
-            nc.vector.tensor_tensor(out=hb[c][:], in0=z[c][:].rearrange("p j t -> p t j"), in1=over_t(ur_sb), op=ALU.mult)
+        def over_tokens(factors):
+            return factors[:].unsqueeze(1).broadcast_to([P, CHUNK, PACK])
 
-        def make_sq(c):
-            nc.scalar.activation(out=sq[c][:], in_=z[c][:].rearrange("p j t -> p t j"), func=ACT.Square)
-
-        def make_ha(c):
-            nc.vector.scalar_tensor_tensor(out=ha[c][:], in0=sq[c][:], scalar=0.5, in1=over_t(us_sb), op0=ALU.mult, op1=ALU.mult)
-
-        def quantize(codes, scales, values):
-            nc.vector.quantize_mx(out=codes.bitcast(FP8X4), scales=scales, in_=values[:].rearrange("p t j -> p (t j)"))
-
-        def second_values(c, first):
-            for i in range(PACK):
-                nc.tensor.matmul_mx(
-                    out=y[c][:, i, :],
-                    lhsT=wd_codes[:, i, :].bitcast(FP8X4), lhsT_scale=wd_sc[:, i, :],
-                    rhs=hb_codes[c][:].bitcast(FP8X4), rhs_scale=hb_scales[c][:],
-                    start=(first and i == 0), stop=(not first and i == PACK - 1),
-                )
-
-        def second_squares(c, first):
-            for i in range(PACK):
-                nc.tensor.matmul_mx(
-                    out=y[c][:, i, :],
-                    lhsT=wb_codes[:, i, :].bitcast(FP4X4), lhsT_scale=wb_sc[:, i, :],
-                    rhs=ha_codes[c][:].bitcast(FP8X4), rhs_scale=ha_scales[c][:],
-                    start=(first and i == 0), stop=(not first and i == PACK - 1),
-                )
-
-        def store_y(c):
-            nc.scalar.copy(out=y_f32[c][:], in_=y[c][:])
-            nc.sync.dma_start(out=out_rows[:, :, c * TC:(c + 1) * TC], in_=y_f32[c][:])
-
-        def round_y_scalar(c):
-            nc.scalar.copy(out=y_bf[c][:], in_=y[c][:].rearrange("p i t -> p t i"))
-
-        def round_y_vector(c):
+        def interleave(side_by_side, rows):
             nc.vector.tensor_copy(
-                out=y_bf[c][:].rearrange("p (a b) i -> p a i b", b=4),
-                in_=y_f32[c][:].rearrange("p i (a b) -> p a i b", b=4),
+                out=side_by_side[:].rearrange("p (a b) j -> p a j b", b=RUN),
+                in_=rows[:].rearrange("p j (a b) -> p a j b", b=RUN),
             )
 
-        def quantize_y(c):
-            cols = slice(c * TC, (c + 1) * TC)
-            quantize(y_codes[:, cols], y_scales[:, cols], y_bf[c])
+        def quantize(codes, scale_bytes, values):
+            nc.vector.quantize_mx(
+                out=codes.bitcast(FP8X4), scales=scale_bytes, in_=values[:].rearrange("p t j -> p (t j)")
+            )
 
-        def store_codes(cols):
-            nc.sync.dma_start(out=out_words[:, cols], in_=y_codes[:, cols].bitcast(I32))
+        def square_z(c):
+            nc.scalar.activation(out=squares[c][:], in_=z[c][:].rearrange("p j t -> p t j"), func=ACT.Square)
+
+        def make_ha(c):
+            nc.vector.scalar_tensor_tensor(
+                out=ha[c][:], in0=squares[c][:], scalar=0.5, in1=over_tokens(us_sb), op0=ALU.mult, op1=ALU.mult
+            )
 
         def make_hb_rows(c):
             for j in range(PACK):
                 nc.scalar.activation(out=hb_rows[c][:, j, :], in_=z[c][:, j, :], func=ACT.Copy, scale=ur_sb[:, j:j + 1])
 
-        def interleave_hb(c):
-            nc.vector.tensor_copy(
-                out=hb[c][:].rearrange("p (a b) j -> p a j b", b=4),
-                in_=hb_rows[c][:].rearrange("p j (a b) -> p a j b", b=4),
+        def make_hb(c):
+            nc.vector.tensor_tensor(
+                out=hb[c][:], in0=z[c][:].rearrange("p j t -> p t j"), in1=over_tokens(ur_sb), op=ALU.mult
             )
 
-        def qa(c):
-            quantize(ha_codes[c][:], ha_scales[c][:], ha[c])
+        def second_layer(c, opens, values, codes, scale_bytes, weights, weight_scales, weight_type):
+            quantize(codes[c][:], scale_bytes[c][:], values[c])
+            if opens and c < LAST:
+                y_banks.append([ps.tile([P, PACK, CHUNK], F32, name="y%d" % c)])
+            elif opens:
+                low = ps.tile([P, PACK // 2, CHUNK], F32, name="y_low")
+                high = ps.tile([P, PACK // 2, CHUNK], F32, name="y_high", tag="z0")
+                y_banks.append([low, high])
+            rows_a_bank = PACK // len(y_banks[c])
+            for i in range(PACK):
+                bank, row = divmod(i, rows_a_bank)
+                nc.tensor.matmul_mx(
+                    out=y_banks[c][bank][:, row, :],
+                    lhsT=weights[:, i, :].bitcast(weight_type),
+                    lhsT_scale=weight_scales[:, i, :],
+                    rhs=codes[c][:].bitcast(FP8X4),
+                    rhs_scale=scale_bytes[c][:],
+                    start=(opens and row == 0),
+                    stop=(not opens and row == rows_a_bank - 1),
+                )
 
-        def qb(c):
-            quantize(hb_codes[c][:], hb_scales[c][:], hb[c])
+        def add_squares(c, opens):
+            second_layer(c, opens, ha, ha_codes, ha_scales, wb_codes, wb_dealt_scales, FP4X4)
 
-        wd_sc = deal(nc.vector.tensor_copy, "wd_sc", planes[:, 6, :], U8, LINE)
-        wb_sc = deal(nc.vector.tensor_copy, "wb_sc", planes[:, 7, :], U8, LINE)
-        wd_codes = deal(nc.vector.tensor_copy, "wd_codes", wd_raw[:], U32, LINE // 4)
-        wb_codes = deal(nc.vector.tensor_copy, "wb_codes", wb_raw[:], U16, LINE // 2)
-        for c in range(CHUNKS):
-            first_layer(c)
-        for c in range(CHUNKS):
-            make_sq(c)
+        def add_values(c, opens):
+            second_layer(c, opens, hb, hb_codes, hb_scales, wd_codes, wd_dealt_scales, FP8X4)
+
+        def store_y(c):
+            rows_a_bank = PACK // len(y_banks[c])
+            for bank, (tile, copy) in enumerate(zip(y_banks[c], (nc.scalar.copy, nc.vector.tensor_copy))):
+                copy(out=y_f32[c][:, bank * rows_a_bank:(bank + 1) * rows_a_bank, :], in_=tile[:])
+            nc.sync.dma_start(out=out_rows[:, :, tokens(c)], in_=y_f32[c][:])
+
+        def quantize_y(c):
+            quantize(y_codes[:, tokens(c)], y_scales[:, tokens(c)], y_bf16[c])
+
+        def store_codes(half):
+            columns = slice(half * HALF, (half + 1) * HALF)
+            queues[half].dma_start(out=out_words[:, columns], in_=y_codes[:, columns].bitcast(I32))
+
+        for c in range(LAST):
+            square_z(c)
             make_hb_rows(c)
             make_ha(c)
             if c > 0:
-                qb(c - 1)
-                second_values(c - 1, False)
-            interleave_hb(c)
-            qa(c)
-            second_squares(c, True)
-        qb(3)
-        second_values(3, False)
+                add_values(c - 1, opens=False)
+            interleave(hb[c], hb_rows[c])
+            add_squares(c, opens=True)
+
+        square_z(LAST)
         store_y(0)
+        make_hb(LAST)
+        add_values(LAST - 1, opens=False)
         store_y(1)
+        nc.scalar.copy(out=y_bf16[0][:], in_=y_banks[0][0][:].rearrange("p i t -> p t i"))
+        make_ha(LAST)
+        add_values(LAST, opens=True)
+        add_squares(LAST, opens=False)
         store_y(2)
-        round_y_vector(0)
-        round_y_vector(1)
+
+        interleave(y_bf16[1], y_f32[1])
         quantize_y(0)
         quantize_y(1)
-        round_y_vector(2)
-        store_y(3)
+        store_codes(0)
+        interleave(y_bf16[2], y_f32[2])
+        store_y(LAST)
         quantize_y(2)
-        store_codes(slice(0, 3 * TC))
-        round_y_vector(3)
-        quantize_y(3)
-        store_codes(slice(3 * TC, T))
-        for q in range(4):
-            queue = nc.sync if q % 2 == 0 else nc.scalar
-            queue.dma_start(out=out_2[0, 4 * q:4 * q + 4, :].bitcast(I32), in_=y_scales[32 * q:32 * q + 4, :].bitcast(I32))
+        interleave(y_bf16[LAST], y_f32[LAST])
+        quantize_y(LAST)
+        store_codes(1)
+        for quadrant in range(P // QUADRANT):
+            queues[quadrant % 2].dma_start(
+                out=out_2[0, 4 * quadrant:4 * quadrant + 4, :].bitcast(I32),
+                in_=y_scales[QUADRANT * quadrant:QUADRANT * quadrant + 4, :].bitcast(I32),
+            )

from contextlib import ExitStack

import concourse.mybir as mybir

K, L, T, R, N = 1024, 512, 512, 512, 512
FLOPS = 2 * T * R * (K + L) + 2 * 2 * N * T * R

F32 = mybir.dt.float32
BF16 = mybir.dt.bfloat16
I32 = mybir.dt.int32
U32 = mybir.dt.uint32
U16 = mybir.dt.uint16
U8 = mybir.dt.uint8
FP8X4 = mybir.dt.float8_e4m3fn_x4
FP4X4 = mybir.dt.float4_e2m1fn_x4
ACT = mybir.ActivationFunctionType
ALU = mybir.AluOpType

P = 128
PACK = 4
WIDTH = 512
CHUNK = 128
CHUNKS = T // CHUNK
LAST = CHUNKS - 1
HALF = T // 2
LINE = 16
RUN = 4
QUADRANT = 32
SCALE_ROWS = 16
WA, XT, WC, XQ, WD, WB, SCALE_PASSES = 0, 2, 4, 5, 6, 7, 8


def tile_mix_hidden_squares_and_values_pl_kernel(
    tc, xt_words, xt_scales, wa_words, wa_scales, xq_words, xq_scales, wc_words, wc_scales,
    us, ur, wb_words, wb_scales, wd_words, wd_scales, out_0, out_1, out_2,
):
    nc = tc.nc
    with ExitStack() as ctx:
        sb = ctx.enter_context(tc.tile_pool(name="sb", bufs=1))
        ps = ctx.enter_context(tc.psum_pool(name="ps", bufs=1))
        ctx.enter_context(tc.manual_schedule())

        def new(name, shape, dtype):
            return sb.tile(shape, dtype, name=name, align_bytes=64)

        def per_chunk(name, shape, dtype, count=CHUNKS):
            return [new("%s%d" % (name, c), shape, dtype) for c in range(count)]

        def load_words(name, shape, dtype, source):
            tile = new(name, shape, dtype)
            nc.sync.dma_start(out=tile[:].bitcast(I32), in_=source.bitcast(I32))
            return tile

        def load_factors(name, source):
            tile = new(name, [P, PACK], F32)
            nc.sync.dma_start(out=tile[:], in_=source.rearrange("(p j) o -> p (j o)", j=PACK))
            return tile

        def load_xt(half):
            source = xt_words[:, :, 2 * HALF * half:2 * HALF * (half + 1)].rearrange("z p b -> p z b")
            return load_words("xt%d" % half, [P, 2, HALF], U16, source)

        def load_xq(half):
            return load_words("xq%d" % half, [P, HALF], U16, xq_words[0, :, 2 * HALF * half:2 * HALF * (half + 1)])

        def deal(copy, name, raw, item_bytes):
            dealt = new(name, [P, PACK, P], raw.dtype)
            run = LINE // item_bytes
            copy(
                out=dealt[:].rearrange("p j (c i) -> p c j i", i=run),
                in_=raw.rearrange("p (c i j) -> p c j i", i=run, j=PACK),
            )
            return dealt

        scales = new("scales", [P, SCALE_PASSES, WIDTH], U8)
        nc.vector.memset(scales[:].rearrange("p s c -> p (s c)").bitcast(U32), 0)
        staged = new("staged", [2 * SCALE_ROWS, SCALE_PASSES, WIDTH], U8)
        queues = (nc.sync, nc.scalar)
        sources = ((WA, wa_scales), (XT, xt_scales), (WC, wc_scales), (XQ, xq_scales), (WD, wd_scales), (WB, wb_scales))
        for number, (place, source) in enumerate(sources):
            queues[number % 2].dma_start(
                out=staged[SCALE_ROWS:, place:place + source.shape[0], :].bitcast(I32),
                in_=source.rearrange("z q c -> q z c").bitcast(I32),
            )
        wa_raw = load_words("wa_raw", [P, 2, WIDTH], U32, wa_words.rearrange("z p n t -> p z (n t)"))
        xt = [load_xt(0)]
        for row in range(4):
            queues[row % 2].dma_start(
                out=scales[row:P:QUADRANT].rearrange("p s c -> p (s c)").bitcast(I32),
                in_=staged[SCALE_ROWS + row::4].rearrange("p s c -> p (s c)").bitcast(I32),
            )
        ur_sb = load_factors("ur_sb", ur)
        us_sb = load_factors("us_sb", us)
        wc_raw = load_words("wc_raw", [P, WIDTH], U32, wc_words[0].rearrange("p n t -> p (n t)"))
        xq = [load_xq(0)]
        wb_raw = load_words("wb_raw", [P, WIDTH], U16, wb_words[0])
        wd_raw = load_words("wd_raw", [P, WIDTH], U32, wd_words[0].rearrange("p n t -> p (n t)"))
        xt.append(load_xt(1))
        xq.append(load_xq(1))

        w_codes = [deal(nc.vector.tensor_copy, "wa_codes%d" % g, wa_raw[:, g, :], 4) for g in range(2)]
        first_scales = new("wa_scales0", [P, PACK, P], U8)
        for j in range(PACK):
            nc.vector.tensor_copy(out=first_scales[:, j, :], in_=scales[:, WA, j::PACK])
        w_scales = [
            first_scales,
            deal(nc.vector.tensor_copy, "wa_scales1", scales[:, WA + 1, :], 1),
            deal(nc.vector.tensor_copy, "wc_scales", scales[:, WC, :], 1),
        ]
        w_codes.append(deal(nc.vector.tensor_copy, "wc_codes", wc_raw[:], 4))
        wb_dealt_scales = deal(nc.vector.tensor_copy, "wb_scales", scales[:, WB, :], 1)
        wd_dealt_scales = deal(nc.vector.tensor_copy, "wd_scales", scales[:, WD, :], 1)
        wb_codes = deal(nc.vector.tensor_copy, "wb_codes", wb_raw[:], 2)
        wd_codes = deal(nc.vector.tensor_copy, "wd_codes", wd_raw[:], 4)

        z = [ps.tile([P, PACK, CHUNK], F32, name="z%d" % c, tag="z%d" % c) for c in range(CHUNKS)]
        for c in range(CHUNKS):
            half, start = divmod(c * CHUNK, HALF)
            in_half = slice(start, start + CHUNK)
            x_codes = (xt[half][:, 0, in_half], xt[half][:, 1, in_half], xq[half][:, in_half])
            for g, x_place in enumerate((XT, XT + 1, XQ)):
                for j in range(PACK):
                    nc.tensor.matmul_mx(
                        out=z[c][:, j, :],
                        lhsT=w_codes[g][:, j, :].bitcast(FP8X4),
                        lhsT_scale=w_scales[g][:, j, :],
                        rhs=x_codes[g].bitcast(FP4X4),
                        rhs_scale=scales[:, x_place, c * CHUNK:(c + 1) * CHUNK],
                        start=(g == 0 and j == 0),
                        stop=(g == 2 and j == PACK - 1),
                    )

        squares = per_chunk("squares", [P, CHUNK, PACK], F32)
        ha = per_chunk("ha", [P, CHUNK, PACK], BF16)
        hb = per_chunk("hb", [P, CHUNK, PACK], BF16)
        hb_rows = per_chunk("hb_rows", [P, PACK, CHUNK], BF16, LAST)
        ha_codes = per_chunk("ha_codes", [P, CHUNK], U32)
        hb_codes = per_chunk("hb_codes", [P, CHUNK], U32)
        ha_scales = per_chunk("ha_scales", [P, CHUNK], U8)
        hb_scales = per_chunk("hb_scales", [P, CHUNK], U8)
        y_f32 = per_chunk("y_f32_", [P, PACK, CHUNK], F32)
        y_bf16 = per_chunk("y_bf16_", [P, CHUNK, PACK], BF16)
        y_codes = new("y_codes", [P, T], U32)
        y_scales = new("y_scales", [P, T], U8)
        y_banks = []
        out_rows = out_0.rearrange("(p i) t -> p i t", i=PACK)
        out_words = out_1[0].rearrange("p t r -> p (t r)").bitcast(I32)

        def tokens(c):
            return slice(c * CHUNK, (c + 1) * CHUNK)

        def over_tokens(factors):
            return factors[:].unsqueeze(1).broadcast_to([P, CHUNK, PACK])

        def interleave(side_by_side, rows):
            nc.vector.tensor_copy(
                out=side_by_side[:].rearrange("p (a b) j -> p a j b", b=RUN),
                in_=rows[:].rearrange("p j (a b) -> p a j b", b=RUN),
            )

        def quantize(codes, scale_bytes, values):
            nc.vector.quantize_mx(
                out=codes.bitcast(FP8X4), scales=scale_bytes, in_=values[:].rearrange("p t j -> p (t j)")
            )

        def square_z(c):
            nc.scalar.activation(out=squares[c][:], in_=z[c][:].rearrange("p j t -> p t j"), func=ACT.Square)

        def make_ha(c):
            nc.vector.scalar_tensor_tensor(
                out=ha[c][:], in0=squares[c][:], scalar=0.5, in1=over_tokens(us_sb), op0=ALU.mult, op1=ALU.mult
            )

        def make_hb_rows(c):
            for j in range(PACK):
                nc.scalar.activation(out=hb_rows[c][:, j, :], in_=z[c][:, j, :], func=ACT.Copy, scale=ur_sb[:, j:j + 1])

        def make_hb(c):
            nc.vector.tensor_tensor(
                out=hb[c][:], in0=z[c][:].rearrange("p j t -> p t j"), in1=over_tokens(ur_sb), op=ALU.mult
            )

        def second_layer(c, opens, values, codes, scale_bytes, weights, weight_scales, weight_type):
            quantize(codes[c][:], scale_bytes[c][:], values[c])
            if opens and c < LAST:
                y_banks.append([ps.tile([P, PACK, CHUNK], F32, name="y%d" % c)])
            elif opens:
                low = ps.tile([P, PACK // 2, CHUNK], F32, name="y_low")
                high = ps.tile([P, PACK // 2, CHUNK], F32, name="y_high", tag="z0")
                y_banks.append([low, high])
            rows_a_bank = PACK // len(y_banks[c])
            for i in range(PACK):
                bank, row = divmod(i, rows_a_bank)
                nc.tensor.matmul_mx(
                    out=y_banks[c][bank][:, row, :],
                    lhsT=weights[:, i, :].bitcast(weight_type),
                    lhsT_scale=weight_scales[:, i, :],
                    rhs=codes[c][:].bitcast(FP8X4),
                    rhs_scale=scale_bytes[c][:],
                    start=(opens and row == 0),
                    stop=(not opens and row == rows_a_bank - 1),
                )

        def add_squares(c, opens):
            second_layer(c, opens, ha, ha_codes, ha_scales, wb_codes, wb_dealt_scales, FP4X4)

        def add_values(c, opens):
            second_layer(c, opens, hb, hb_codes, hb_scales, wd_codes, wd_dealt_scales, FP8X4)

        def store_y(c):
            rows_a_bank = PACK // len(y_banks[c])
            for bank, (tile, copy) in enumerate(zip(y_banks[c], (nc.scalar.copy, nc.vector.tensor_copy))):
                copy(out=y_f32[c][:, bank * rows_a_bank:(bank + 1) * rows_a_bank, :], in_=tile[:])
            nc.sync.dma_start(out=out_rows[:, :, tokens(c)], in_=y_f32[c][:])

        def quantize_y(c):
            quantize(y_codes[:, tokens(c)], y_scales[:, tokens(c)], y_bf16[c])

        def store_codes(half):
            columns = slice(half * HALF, (half + 1) * HALF)
            queues[half].dma_start(out=out_words[:, columns], in_=y_codes[:, columns].bitcast(I32))

        for c in range(LAST):
            square_z(c)
            make_hb_rows(c)
            make_ha(c)
            if c > 0:
                add_values(c - 1, opens=False)
            interleave(hb[c], hb_rows[c])
            add_squares(c, opens=True)

        square_z(LAST)
        store_y(0)
        make_hb(LAST)
        add_values(LAST - 1, opens=False)
        store_y(1)
        nc.scalar.copy(out=y_bf16[0][:], in_=y_banks[0][0][:].rearrange("p i t -> p t i"))
        make_ha(LAST)
        add_values(LAST, opens=True)
        add_squares(LAST, opens=False)
        store_y(2)

        interleave(y_bf16[1], y_f32[1])
        quantize_y(0)
        quantize_y(1)
        store_codes(0)
        interleave(y_bf16[2], y_f32[2])
        store_y(LAST)
        quantize_y(2)
        interleave(y_bf16[LAST], y_f32[LAST])
        quantize_y(LAST)
        store_codes(1)
        for quadrant in range(P // QUADRANT):
            queues[quadrant % 2].dma_start(
                out=out_2[0, 4 * quadrant:4 * quadrant + 4, :].bitcast(I32),
                in_=y_scales[QUADRANT * quadrant:QUADRANT * quadrant + 4, :].bitcast(I32),
            )
